import numpy as np, ml_dtypes
CORES = [22,38,54,62,70,110,23,39,55,63,71,111]
N = 12
DEG, TK, TIMES = 3, 128, 2
MASK = [[11,0,1],[0,1,2],[1,2,3],[2,3,4],[3,4,5],[4,5,6],[5,6,7],[6,7,8],[7,8,9],[8,9,10],[9,10,11],[10,11,0]]
def setup_inputs(rng):
    return {"x": rng.standard_normal((N, 128, TK), dtype=np.float32).astype(ml_dtypes.bfloat16), "w": (rng.standard_normal((N, 128, DEG * 128), dtype=np.float32) / np.float32(np.sqrt(128 * DEG / 2))).astype(ml_dtypes.bfloat16)}
def setup_inputs_big(rng):
    d = setup_inputs(rng)
    for k in ("x",): d[k] = (d[k].astype(np.float32) * 1048576.0).astype(d[k].dtype)
    return d
def setup_inputs_small(rng):
    d = setup_inputs(rng)
    for k in ("x",): d[k] = (d[k].astype(np.float32) * (1 / 1048576.0)).astype(d[k].dtype)
    return d
def setup_inputs_apart(rng):
    d = setup_inputs(rng)
    f = (10.0 ** rng.permutation(np.linspace(-1.5, 1.5, N))).astype(np.float32).reshape(N, 1, 1)
    for k in ("x",): d[k] = (d[k].astype(np.float32) * f).astype(d[k].dtype)
    return d
def reference(x, w):
    X, W = x.astype(np.float64), w.astype(np.float64)
    h = list(X)
    for _ in range(TIMES):
        h = [sum(W[r][:, 128 * i:128 * i + 128].T @ h[j] for i, j in enumerate(MASK[r])) for r in range(N)]
    return {"y": np.stack(h).astype(ml_dtypes.bfloat16)}

@@ -1,0 +1,104 @@
+from concourse.bass import DstId, RemoteDMATransfer
+
+TK = 128
+DEG = 3
+
+SCRATCH = {
+    "xs": ("sbuf", [128, TK], "bfloat16"),
+    "ws": ("sbuf", [128, DEG * 128], "bfloat16"),
+    "land1": ("sbuf", [128, DEG * TK], "bfloat16"),
+    "land2": ("sbuf", [128, DEG * TK], "bfloat16"),
+    "h1": ("sbuf", [128, TK], "bfloat16"),
+    "ys": ("sbuf", [128, TK], "bfloat16"),
+    "ps1": ("psum", [128, 512], "float32"),
+    "ps2": ("psum", [128, 512], "float32"),
+}
+SEMAPHORES = ["ldx", "ldw", "arr1", "arr2", "sent", "mm1", "cp1", "mm2", "cp2", "st"]
+
+
+def _engines(topo, core, dsts):
+    common = topo.mask(core, dsts[0])
+    for d in dsts[1:]:
+        common &= topo.mask(core, d)
+    bits = [b for b in range(common.bit_length()) if (common >> b) & 1]
+    n = 1
+    while n * 2 <= len(bits) and 128 % (n * 2) == 0:
+        n *= 2
+    m = 0
+    for b in bits[:n]:
+        m |= 1 << b
+    return m, n
+
+
+def rank_program(g, core, T, topo):
+    rank = T.rank_of(core)
+    if rank is None:
+        return
+    mask_tab = T.tables["MASK"]
+    cores = T.cores
+    n_ranks = len(cores)
+    S = T.sem
+
+    readers = [(cores[r], i) for r in range(n_ranks) for i, j in enumerate(mask_tab[r]) if j == rank and r != rank]
+    home = [i for i, j in enumerate(mask_tab[rank]) if j == rank]
+    away = [i for i, j in enumerate(mask_tab[rank]) if j != rank]
+    for c, _ in readers:
+        assert topo.may_write(core, c)
+    emask, n_eng = _engines(topo, core, [c for c, _ in readers])
+    arrive = 0
+    for i in away:
+        src = cores[mask_tab[rank][i]]
+        src_rank = mask_tab[rank][i]
+        src_readers = [cores[r] for r in range(n_ranks) for j in mask_tab[r] if j == src_rank and r != src_rank]
+        arrive += _engines(topo, src, src_readers)[1]
+
+    def tile(i):
+        return T.ws[:, 128 * i:128 * (i + 1)]
+
+    def slot(buf, i):
+        return buf[:, TK * i:TK * (i + 1)]
+
+    def send(src, land, sem):
+        ids = []
+        for c, _ in readers:
+            rid, pid, _se = topo.addr(c)
+            ids.append(DstId(rid=rid, pnc=pid))
+        g.remote_dma_fused(
+            [RemoteDMATransfer(dst_ids=ids, dma_engine_mask=emask, remote_sem=sem,
+                               srcs=[src[:, :]], dsts=[slot(land, i) for _, i in readers], alu_op=0)],
+            local_sem=S.sent)
+
+    def replace(ps, h_home, land, arr_sem, done_sem):
+        terms = len(home) + len(away)
+        k = 0
+        for i in home:
+            k += 1
+            mm = g.tensor.matmul(ps[:, 0:TK], tile(i), h_home[:, :], start=(k == 1), stop=(k == terms))
+        g.tensor.wait_ge(arr_sem, arrive)
+        for i in away:
+            k += 1
+            mm = g.tensor.matmul(ps[:, 0:TK], tile(i), slot(land, i), start=(k == 1), stop=(k == terms))
+        mm.then_inc(done_sem, 1)
+
+    g.sync.dma_start(T.xs[:, :], T.x[:, :]).then_inc(S.ldx, 16)
+    g.sync.dma_start(T.ws[:, :], T.w[:, :]).then_inc(S.ldw, 16)
+
+    g.wait_ge(S.ldx, 16)
+    send(T.xs, T.land1, S.arr1)
+    g.tensor.wait_ge(S.ldx, 16)
+    g.tensor.wait_ge(S.ldw, 16)
+    replace(T.ps1, T.xs, T.land1, S.arr1, S.mm1)
+    g.vector.wait_ge(S.mm1, 1)
+    g.vector.tensor_copy(T.h1[:, :], T.ps1[:, 0:TK]).then_inc(S.cp1, 1)
+
+    g.wait_ge(S.cp1, 1)
+    send(T.h1, T.land2, S.arr2)
+    g.tensor.wait_ge(S.cp1, 1)
+    replace(T.ps2, T.h1, T.land2, S.arr2, S.mm2)
+    g.vector.wait_ge(S.mm2, 1)
+    g.vector.tensor_copy(T.ys[:, :], T.ps2[:, 0:TK]).then_inc(S.cp2, 1)
+
+    g.sync.wait_ge(S.cp2, 1)
+    g.sync.dma_start(T.y[:, :], T.ys[:, :]).then_inc(S.st, 16)
+    g.sync.wait_ge(S.st, 16)
+    g.wait_ge(S.sent, 2 * n_eng)

@@ -2,6 +2,7 @@ from concourse.bass import DstId, RemoteDMATransfer
 
 TK = 128
 DEG = 3
+HALVES = ((0, TK // 2), (TK // 2, TK))
 
 SCRATCH = {
     "xs": ("sbuf", [128, TK], "bfloat16"),
@@ -10,24 +11,39 @@ SCRATCH = {
     "land2": ("sbuf", [128, DEG * TK], "bfloat16"),
     "h1": ("sbuf", [128, TK], "bfloat16"),
     "ys": ("sbuf", [128, TK], "bfloat16"),
-    "ps1": ("psum", [128, 512], "float32"),
-    "ps2": ("psum", [128, 512], "float32"),
+    "ps10": ("psum", [128, 512], "float32"),
+    "ps11": ("psum", [128, 512], "float32"),
+    "ps20": ("psum", [128, 512], "float32"),
+    "ps21": ("psum", [128, 512], "float32"),
 }
-SEMAPHORES = ["ldx", "ldw", "arr1", "arr2", "sent", "mm1", "cp1", "mm2", "cp2", "st"]
+SEMAPHORES = (["ldx0", "ldx1", "ldw", "sent", "st0", "st1"]
+              + ["mm%d%d" % (t, p) for t in (1, 2) for p in (0, 1)]
+              + ["cp%d%d" % (t, p) for t in (1, 2) for p in (0, 1)]
+              + ["arr%d%d%d" % (t, p, i) for t in (1, 2) for p in (0, 1) for i in range(DEG)])
 
 
-def _engines(topo, core, dsts):
+def _shares(topo, core, dsts):
     common = topo.mask(core, dsts[0])
     for d in dsts[1:]:
         common &= topo.mask(core, d)
     bits = [b for b in range(common.bit_length()) if (common >> b) & 1]
     n = 1
-    while n * 2 <= len(bits) and 128 % (n * 2) == 0:
+    while n * 2 * len(dsts) <= len(bits) and 128 % (n * 2) == 0:
         n *= 2
-    m = 0
-    for b in bits[:n]:
-        m |= 1 << b
-    return m, n
+    masks = []
+    for k in range(len(dsts)):
+        m = 0
+        for b in bits[k * n:(k + 1) * n]:
+            m |= 1 << b
+        masks.append(m)
+    return masks, n
+
+
+def _hops(topo, a, b):
+    ca, cb = topo.chip(a), topo.chip(b)
+    if ca == cb:
+        return 0
+    return 1 if (topo.mates(ca, cb) or topo.same_plane(ca, cb)) else 2
 
 
 def rank_program(g, core, T, topo):
@@ -39,66 +55,95 @@ def rank_program(g, core, T, topo):
     n_ranks = len(cores)
     S = T.sem
 
-    readers = [(cores[r], i) for r in range(n_ranks) for i, j in enumerate(mask_tab[r]) if j == rank and r != rank]
+    def readers_of(j):
+        return [(cores[r], i) for r in range(n_ranks) for i, k in enumerate(mask_tab[r]) if k == j and r != j]
+
+    readers = readers_of(rank)
     home = [i for i, j in enumerate(mask_tab[rank]) if j == rank]
     away = [i for i, j in enumerate(mask_tab[rank]) if j != rank]
+    away.sort(key=lambda i: _hops(topo, cores[mask_tab[rank][i]], core))
     for c, _ in readers:
         assert topo.may_write(core, c)
-    emask, n_eng = _engines(topo, core, [c for c, _ in readers])
-    arrive = 0
+    emasks, n_eng = _shares(topo, core, [c for c, _ in readers])
+    arrive = {}
     for i in away:
-        src = cores[mask_tab[rank][i]]
-        src_rank = mask_tab[rank][i]
-        src_readers = [cores[r] for r in range(n_ranks) for j in mask_tab[r] if j == src_rank and r != src_rank]
-        arrive += _engines(topo, src, src_readers)[1]
+        j = mask_tab[rank][i]
+        arrive[i] = _shares(topo, cores[j], [c for c, _ in readers_of(j)])[1]
 
     def tile(i):
         return T.ws[:, 128 * i:128 * (i + 1)]
 
-    def slot(buf, i):
-        return buf[:, TK * i:TK * (i + 1)]
+    def part(buf, p, i=0):
+        lo, hi = HALVES[p]
+        return buf[:, TK * i + lo:TK * i + hi]
 
-    def send(src, land, sem):
-        ids = []
-        for c, _ in readers:
+    def send(t, p, src, land):
+        trs = []
+        for (c, i), m in zip(readers, emasks):
             rid, pid, _se = topo.addr(c)
-            ids.append(DstId(rid=rid, pnc=pid))
-        g.remote_dma_fused(
-            [RemoteDMATransfer(dst_ids=ids, dma_engine_mask=emask, remote_sem=sem,
-                               srcs=[src[:, :]], dsts=[slot(land, i) for _, i in readers], alu_op=0)],
-            local_sem=S.sent)
+            trs.append(RemoteDMATransfer(dst_ids=[DstId(rid=rid, pnc=pid)], dma_engine_mask=m,
+                                         remote_sem=S["arr%d%d%d" % (t, p, i)],
+                                         srcs=[part(src, p)], dsts=[part(land, p, i)], alu_op=0))
+        g.remote_dma_fused(trs, local_sem=S.sent)
 
-    def replace(ps, h_home, land, arr_sem, done_sem):
-        terms = len(home) + len(away)
-        k = 0
-        for i in home:
-            k += 1
-            mm = g.tensor.matmul(ps[:, 0:TK], tile(i), h_home[:, :], start=(k == 1), stop=(k == terms))
-        g.tensor.wait_ge(arr_sem, arrive)
+    width = HALVES[0][1] - HALVES[0][0]
+    terms = len(home) + len(away)
+
+    def home_terms(t, p, h_home):
+        ps = T["ps%d%d" % (t, p)]
+        for k, i in enumerate(home):
+            g.tensor.matmul(ps[:, 0:width], tile(i), part(h_home, p), start=(k == 0), stop=(k + 1 == terms))
+
+    def away_terms(t, p, land):
+        ps = T["ps%d%d" % (t, p)]
+        k = len(home)
+        mm = None
         for i in away:
+            g.tensor.wait_ge(S["arr%d%d%d" % (t, p, i)], arrive[i])
             k += 1
-            mm = g.tensor.matmul(ps[:, 0:TK], tile(i), slot(land, i), start=(k == 1), stop=(k == terms))
-        mm.then_inc(done_sem, 1)
+            mm = g.tensor.matmul(ps[:, 0:width], tile(i), part(land, p, i), start=(k == 1), stop=(k == terms))
+        mm.then_inc(S["mm%d%d" % (t, p)], 1)
 
-    g.sync.dma_start(T.xs[:, :], T.x[:, :]).then_inc(S.ldx, 16)
+    def narrow(t, p, out):
+        g.vector.wait_ge(S["mm%d%d" % (t, p)], 1)
+        g.vector.tensor_copy(part(out, p), T["ps%d%d" % (t, p)][:, 0:width]).then_inc(S["cp%d%d" % (t, p)], 1)
+
+    g.sync.dma_start(part(T.xs, 0), part(T.x, 0)).then_inc(S.ldx0, 16)
+    g.scalar.dma_start(part(T.xs, 1), part(T.x, 1)).then_inc(S.ldx1, 16)
     g.sync.dma_start(T.ws[:, :], T.w[:, :]).then_inc(S.ldw, 16)
 
-    g.wait_ge(S.ldx, 16)
-    send(T.xs, T.land1, S.arr1)
-    g.tensor.wait_ge(S.ldx, 16)
+    g.wait_ge(S.ldx0, 16)
+    send(1, 0, T.xs, T.land1)
+    g.wait_ge(S.ldx1, 16)
+    send(1, 1, T.xs, T.land1)
+    g.wait_ge(S.cp10, 1)
+    send(2, 0, T.h1, T.land2)
+    g.wait_ge(S.cp11, 1)
+    send(2, 1, T.h1, T.land2)
+
     g.tensor.wait_ge(S.ldw, 16)
-    replace(T.ps1, T.xs, T.land1, S.arr1, S.mm1)
-    g.vector.wait_ge(S.mm1, 1)
-    g.vector.tensor_copy(T.h1[:, :], T.ps1[:, 0:TK]).then_inc(S.cp1, 1)
+    g.tensor.wait_ge(S.ldx0, 16)
+    home_terms(1, 0, T.xs)
+    g.tensor.wait_ge(S.ldx1, 16)
+    home_terms(1, 1, T.xs)
+    away_terms(1, 0, T.land1)
+    g.tensor.wait_ge(S.cp10, 1)
+    home_terms(2, 0, T.h1)
+    away_terms(1, 1, T.land1)
+    g.tensor.wait_ge(S.cp11, 1)
+    home_terms(2, 1, T.h1)
+    away_terms(2, 0, T.land2)
+    away_terms(2, 1, T.land2)
 
-    g.wait_ge(S.cp1, 1)
-    send(T.h1, T.land2, S.arr2)
-    g.tensor.wait_ge(S.cp1, 1)
-    replace(T.ps2, T.h1, T.land2, S.arr2, S.mm2)
-    g.vector.wait_ge(S.mm2, 1)
-    g.vector.tensor_copy(T.ys[:, :], T.ps2[:, 0:TK]).then_inc(S.cp2, 1)
+    narrow(1, 0, T.h1)
+    narrow(1, 1, T.h1)
+    narrow(2, 0, T.ys)
+    narrow(2, 1, T.ys)
 
-    g.sync.wait_ge(S.cp2, 1)
-    g.sync.dma_start(T.y[:, :], T.ys[:, :]).then_inc(S.st, 16)
-    g.sync.wait_ge(S.st, 16)
-    g.wait_ge(S.sent, 2 * n_eng)
+    g.sync.wait_ge(S.cp20, 1)
+    g.sync.dma_start(part(T.y, 0), part(T.ys, 0)).then_inc(S.st0, 16)
+    g.scalar.wait_ge(S.cp21, 1)
+    g.scalar.dma_start(part(T.y, 1), part(T.ys, 1)).then_inc(S.st1, 16)
+    g.sync.wait_ge(S.st0, 16)
+    g.scalar.wait_ge(S.st1, 16)
+    g.wait_ge(S.sent, 4 * n_eng * len(readers))

from concourse.bass import DstId, RemoteDMATransfer

TK = 128
DEG = 3
HALVES = ((0, TK // 2), (TK // 2, TK))

SCRATCH = {
    "xs": ("sbuf", [128, TK], "bfloat16"),
    "ws": ("sbuf", [128, DEG * 128], "bfloat16"),
    "land1": ("sbuf", [128, DEG * TK], "bfloat16"),
    "land2": ("sbuf", [128, DEG * TK], "bfloat16"),
    "h1": ("sbuf", [128, TK], "bfloat16"),
    "ys": ("sbuf", [128, TK], "bfloat16"),
    "ps10": ("psum", [128, 512], "float32"),
    "ps11": ("psum", [128, 512], "float32"),
    "ps20": ("psum", [128, 512], "float32"),
    "ps21": ("psum", [128, 512], "float32"),
}
SEMAPHORES = (["ldx0", "ldx1", "ldw", "sent", "st0", "st1"]
              + ["mm%d%d" % (t, p) for t in (1, 2) for p in (0, 1)]
              + ["cp%d%d" % (t, p) for t in (1, 2) for p in (0, 1)]
              + ["arr%d%d%d" % (t, p, i) for t in (1, 2) for p in (0, 1) for i in range(DEG)])


def _shares(topo, core, dsts):
    common = topo.mask(core, dsts[0])
    for d in dsts[1:]:
        common &= topo.mask(core, d)
    bits = [b for b in range(common.bit_length()) if (common >> b) & 1]
    n = 1
    while n * 2 * len(dsts) <= len(bits) and 128 % (n * 2) == 0:
        n *= 2
    masks = []
    for k in range(len(dsts)):
        m = 0
        for b in bits[k * n:(k + 1) * n]:
            m |= 1 << b
        masks.append(m)
    return masks, n


def _hops(topo, a, b):
    ca, cb = topo.chip(a), topo.chip(b)
    if ca == cb:
        return 0
    return 1 if (topo.mates(ca, cb) or topo.same_plane(ca, cb)) else 2


def rank_program(g, core, T, topo):
    rank = T.rank_of(core)
    if rank is None:
        return
    mask_tab = T.tables["MASK"]
    cores = T.cores
    n_ranks = len(cores)
    S = T.sem

    def readers_of(j):
        return [(cores[r], i) for r in range(n_ranks) for i, k in enumerate(mask_tab[r]) if k == j and r != j]

    readers = readers_of(rank)
    home = [i for i, j in enumerate(mask_tab[rank]) if j == rank]
    away = [i for i, j in enumerate(mask_tab[rank]) if j != rank]
    away.sort(key=lambda i: _hops(topo, cores[mask_tab[rank][i]], core))
    for c, _ in readers:
        assert topo.may_write(core, c)
    emasks, n_eng = _shares(topo, core, [c for c, _ in readers])
    arrive = {}
    for i in away:
        j = mask_tab[rank][i]
        arrive[i] = _shares(topo, cores[j], [c for c, _ in readers_of(j)])[1]

    def tile(i):
        return T.ws[:, 128 * i:128 * (i + 1)]

    def part(buf, p, i=0):
        lo, hi = HALVES[p]
        return buf[:, TK * i + lo:TK * i + hi]

    def send(t, p, src, land):
        trs = []
        for (c, i), m in zip(readers, emasks):
            rid, pid, _se = topo.addr(c)
            trs.append(RemoteDMATransfer(dst_ids=[DstId(rid=rid, pnc=pid)], dma_engine_mask=m,
                                         remote_sem=S["arr%d%d%d" % (t, p, i)],
                                         srcs=[part(src, p)], dsts=[part(land, p, i)], alu_op=0))
        g.remote_dma_fused(trs, local_sem=S.sent)

    width = HALVES[0][1] - HALVES[0][0]
    terms = len(home) + len(away)

    def home_terms(t, p, h_home):
        ps = T["ps%d%d" % (t, p)]
        for k, i in enumerate(home):
            g.tensor.matmul(ps[:, 0:width], tile(i), part(h_home, p), start=(k == 0), stop=(k + 1 == terms))

    def away_terms(t, p, land):
        ps = T["ps%d%d" % (t, p)]
        k = len(home)
        mm = None
        for i in away:
            g.tensor.wait_ge(S["arr%d%d%d" % (t, p, i)], arrive[i])
            k += 1
            mm = g.tensor.matmul(ps[:, 0:width], tile(i), part(land, p, i), start=(k == 1), stop=(k == terms))
        mm.then_inc(S["mm%d%d" % (t, p)], 1)

    def narrow(t, p, out):
        g.vector.wait_ge(S["mm%d%d" % (t, p)], 1)
        g.vector.tensor_copy(part(out, p), T["ps%d%d" % (t, p)][:, 0:width]).then_inc(S["cp%d%d" % (t, p)], 1)

    g.sync.dma_start(part(T.xs, 0), part(T.x, 0)).then_inc(S.ldx0, 16)
    g.scalar.dma_start(part(T.xs, 1), part(T.x, 1)).then_inc(S.ldx1, 16)
    g.sync.dma_start(T.ws[:, :], T.w[:, :]).then_inc(S.ldw, 16)

    g.wait_ge(S.ldx0, 16)
    send(1, 0, T.xs, T.land1)
    g.wait_ge(S.ldx1, 16)
    send(1, 1, T.xs, T.land1)
    g.wait_ge(S.cp10, 1)
    send(2, 0, T.h1, T.land2)
    g.wait_ge(S.cp11, 1)
    send(2, 1, T.h1, T.land2)

    g.tensor.wait_ge(S.ldw, 16)
    g.tensor.wait_ge(S.ldx0, 16)
    home_terms(1, 0, T.xs)
    g.tensor.wait_ge(S.ldx1, 16)
    home_terms(1, 1, T.xs)
    away_terms(1, 0, T.land1)
    g.tensor.wait_ge(S.cp10, 1)
    home_terms(2, 0, T.h1)
    away_terms(1, 1, T.land1)
    g.tensor.wait_ge(S.cp11, 1)
    home_terms(2, 1, T.h1)
    away_terms(2, 0, T.land2)
    away_terms(2, 1, T.land2)

    narrow(1, 0, T.h1)
    narrow(1, 1, T.h1)
    narrow(2, 0, T.ys)
    narrow(2, 1, T.ys)

    g.sync.wait_ge(S.cp20, 1)
    g.sync.dma_start(part(T.y, 0), part(T.ys, 0)).then_inc(S.st0, 16)
    g.scalar.wait_ge(S.cp21, 1)
    g.scalar.dma_start(part(T.y, 1), part(T.ys, 1)).then_inc(S.st1, 16)
    g.sync.wait_ge(S.st0, 16)
    g.scalar.wait_ge(S.st1, 16)
    g.wait_ge(S.sent, 4 * n_eng * len(readers))
